import numpy as np
import ml_dtypes


def mxq(x, axis, fmt="e4m3"):
    dtype, down = {"e4m3": (ml_dtypes.float8_e4m3fn, 7), "e5m2": (ml_dtypes.float8_e5m2, 14)}[fmt]
    v = np.moveaxis(np.asarray(x, np.float32).astype(ml_dtypes.bfloat16).astype(np.float64), axis, -1)
    blocks = v.reshape(v.shape[:-1] + (-1, 32))
    amax = np.abs(blocks).max(-1, keepdims=True)
    byte = np.maximum(np.where(amax > 0, np.frexp(amax)[1] - 1 + 127, 0) - down, 1)
    scale = np.exp2(byte - 127.0)
    codes = (blocks / scale).astype(np.float32).astype(dtype).astype(np.float64)
    return np.moveaxis((codes * scale).reshape(v.shape), -1, axis)


WIDE = False


def mx_kscale(k):
    if not WIDE:
        return np.ones(k)
    levels = np.array([30, -30])
    if k % 512:
        return np.exp2(np.random.permutation(np.resize(levels, k // 32))).repeat(32)
    a = np.empty((k // 512, 16))
    for p in range(k // 512):
        a[p, :8] = np.random.permutation(np.resize(levels, 8))
        for g in range(8):
            far = levels[np.abs(levels - a[p, g]) >= 10]
            a[p, g + 8] = far[np.random.randint(len(far))]
    return np.exp2(a.ravel()).repeat(32)


BF16 = ml_dtypes.bfloat16


def bf(x):
    return np.asarray(x, np.float32).astype(BF16)


def f64(x):
    return np.asarray(x).astype(np.float64)


E2M1 = np.array([0.0, 0.5, 1.0, 1.5, 2.0, 3.0, 4.0, 6.0, -0.0, -0.5, -1.0, -1.5, -2.0, -3.0, -4.0, -6.0])


def pack_weight(w, fmt):
    k, n = w.shape
    w = f64(bf(w)).reshape(k // 32, 32, n)
    amax = np.abs(w).max(1)
    if fmt in ("e4m3", "e5m2"):
        byte = np.frexp(amax)[1] - 1 + 127 - (7 if fmt == "e4m3" else 14)
    else:
        mant, ex = np.frexp(amax / 6.0)
        byte = np.where(mant > 0.5, ex, ex - 1) + 127
    byte = np.clip(np.where(amax > 0, byte, 1), 1, 254)
    scaled = (w * np.exp2(127.0 - byte)[:, None, :]).reshape(k, n).astype(np.float32)
    by_word = np.ascontiguousarray(scaled.reshape(k // 512, 128, 4, n).transpose(0, 1, 3, 2))
    if fmt in ("e4m3", "e5m2"):
        words = by_word.astype(ml_dtypes.float8_e4m3fn if fmt == "e4m3" else ml_dtypes.float8_e5m2).view(np.uint8)
    else:
        c = by_word.astype(ml_dtypes.float4_e2m1fn).view(np.uint8) & 0xF
        words = c[..., 0::2] | (c[..., 1::2] << 4)
    return np.ascontiguousarray(words), np.ascontiguousarray(byte.astype(np.uint8).reshape(k // 512, 16, n))


def unpack_weight(words, scales, fmt):
    g, p, n, _ = words.shape
    if fmt in ("e4m3", "e5m2"):
        vals = np.ascontiguousarray(words).view(ml_dtypes.float8_e4m3fn if fmt == "e4m3" else ml_dtypes.float8_e5m2).astype(np.float64)
    else:
        nib = np.empty((g, p, n, 4), np.uint8)
        nib[..., 0::2] = words & 0xF
        nib[..., 1::2] = words >> 4
        vals = E2M1[nib]
    vals = vals * np.repeat(np.exp2(scales.astype(np.float64) - 127.0), 8, axis=1)[..., None]
    return vals.transpose(0, 1, 3, 2).reshape(g * 512, n)


S, A, F, L = 2048, 1024, 1024, 2048


def setup_inputs():
    s = mx_kscale(S)
    v = mx_kscale(L)
    G = np.random.standard_normal((S, F)) * np.exp(0.5 * np.random.standard_normal((S, F)))
    G_words, G_scales = pack_weight(G * s[:, None], "e5m2")
    return {
        "rec": bf(np.random.standard_normal((A, S)) / np.sqrt(S) / s),
        "g_words": G_words,
        "g_scales": G_scales,
        "pred": bf(np.random.standard_normal((A, L)) / np.sqrt(L) / v),
        "hist": bf(np.random.standard_normal((F, L)) * v),
        "cal": bf(1 + 0.1 * np.random.standard_normal(A)),
        "lo": bf(-2 + 0.2 * np.random.standard_normal(A)),
        "hi": bf(2 + 0.2 * np.random.standard_normal(A)),
    }


def reference(rec, g_words, g_scales, pred, hist, cal, lo, hi):
    G = unpack_weight(g_words, g_scales, "e5m2")
    corr = mxq(f64(rec), 1, "e4m3") @ G
    ahead = mxq(f64(pred), 1, "e4m3") @ mxq(f64(hist), 1, "e4m3").T
    drive = (corr + ahead) * f64(cal)[:, None]
    return np.minimum(np.maximum(drive, f64(lo)[:, None]), f64(hi)[:, None])

@@ -1,0 +1,253 @@
+from contextlib import ExitStack
+
+import concourse.mybir as mybir
+from concourse.masks import make_identity
+
+S, A, F, L = 2048, 1024, 1024, 2048
+FLOPS = 2 * A * F * (S + L)
+
+F32 = mybir.dt.float32
+BF16 = mybir.dt.bfloat16
+I32 = mybir.dt.int32
+U32 = mybir.dt.uint32
+U8 = mybir.dt.uint8
+E4M3X4 = mybir.dt.float8_e4m3fn_x4
+E5M2X4 = mybir.dt.float8_e5m2_x4
+ALU = mybir.AluOpType
+ACT = mybir.ActivationFunctionType
+
+P = 128
+PASSES = 4
+TILES = 8
+N = 512
+T_BANKS = 4
+A_BANKS = 4
+RE_BUFS = 8
+GR_BUFS = 6
+
+LOADS = "R0a R0b R1 g00 g01 s0 g02 g03 H0 R2 R3 H1 H2 H3 P0 P1 P2 P3 H4 H5 H6 H7 s1 G1 R4 P4 R5 P5 R6 P6 R7 P7".split()
+PE_ORDER = "R0 R1 R00 R10 H0 R2 R3 R20 H1 H2 H3 R30 P0 P1 P2 P00 P3 H4 P10 P20 H5 H6 H7 P30 R01 R11 R21 R4 P4 P01 P11 P21 R31 P31 R5 P5 R40 P40 R41 P41 R6 P6 R50 P50 R51 P51 R7 P7 R60 P60 R61 P61 R70 P70 R71 P71".split()
+DIRECT = set("R0 R1 R2 R3".split())
+V_ORDER = "qR00 qR01 qR10 qR11 reH00 reH01 qH00 qH01 qR20 reH10 qR21 reH11 qR30 reH20 qR31 reH21 reH30 reH31 qH10 reP00 qH11 reP01 qH20 reP10 qH21 qH30 reP11 qH31 reP20 reP21 qP00 reP30 qP01 reP31 qP10 reH40 qP11 reH41 qP20 qP21 reH50 reH51 qP30 reH60 qP31 reH61 qH40 reH70 qH41 reH71 cl00 cl10 cl20 qH50 qH51 qH60 reR40 qH61 reR41 qH70 reP40 qH71 reP41 reR50 reR51 cl30 reP50 reP51 reR60 reR61 qR40 reP60 qR41 reP61 qP40 qP41 cl01 cl11 cl21 reR70 reR71 reP70 qR50 reP71 qR51 cl31 qP50 qP51 cl40 cl41 qR60 qR61 qP60 qP61 cl50 cl51 qR70 qR71 qP70 qP71 cl60 cl61 cl70 cl71".split()
+S_ORDER = "evR00 evR01 cal evR10 evR11 evH00 evH01 evR20 evR21 evR30 evR31 evH10 evH11 evH20 evH21 evH30 evH31 evP00 evP01 evP10 evP11 evP20 evP21 evP30 evP31 evH40 evH41 ep00 ep10 ep20 evH50 evH51 evH60 evH61 evH70 evH71 ep30 evR40 evR41 evP40 evP41 ep01 ep11 ep21 ep31 evR50 evR51 evP50 evP51 ep40 ep41 evR60 evR61 evP60 evP61 ep50 ep51 evR70 evR71 evP70 evP71 ep60 ep61 ep70 ep71".split()
+
+
+def tile_adaptive_optics_reconstructor_e4_kernel(tc, rec, g_words, g_scales, pred, hist, cal, lo, hi, out):
+    nc = tc.nc
+    rows = {
+        "R": rec.rearrange("(p i) k -> i p k", i=TILES),
+        "P": pred.rearrange("(p i) k -> i p k", i=TILES),
+        "H": hist.rearrange("(i p) k -> i p k", p=P),
+    }
+    out_rows = out.rearrange("(p i) f -> i p f", i=TILES)
+    g_by_part = g_words.rearrange("g p n t -> p g (n t)")
+    g_scale_rows = g_scales.rearrange("g (q r) n -> r q g n", r=4)
+
+    with ExitStack() as ctx:
+        keep = ctx.enter_context(tc.tile_pool(name="keep", bufs=1))
+        psum = ctx.enter_context(tc.psum_pool(name="psum", bufs=1))
+        ctx.enter_context(tc.manual_schedule())
+
+        ident = keep.tile([P, P], F32, name="ident")
+        make_identity(nc, ident[:])
+        vec = {}
+        for key, src in (("cal", cal), ("lo", lo), ("hi", hi)):
+            vec[key] = keep.tile([P, TILES], BF16, name=key)
+            nc.gpsimd.dma_start(out=vec[key][:], in_=src.rearrange("(p i) -> p i", i=TILES))
+        cal32 = keep.tile([P, TILES], F32, name="cal32")
+
+        g_codes, g_sc, h_codes, h_sc = [], [], [], []
+        for h in range(2):
+            g_codes.append(keep.tile([P, PASSES, N], U32, name="gc%d" % h, align_bytes=64))
+            g_sc.append(keep.tile([P, PASSES, N], U8, name="gs%d" % h, align_bytes=64))
+            h_codes.append(keep.tile([P, PASSES, N], U32, name="hc%d" % h, align_bytes=64))
+            h_sc.append(keep.tile([P, PASSES, N], U8, name="hs%d" % h, align_bytes=64))
+            nc.vector.memset(g_sc[h][:].bitcast(U32), 0)
+
+        raw = {}
+        for name in LOADS:
+            if name[0] == "s":
+                h = int(name[1])
+                for r in range(4):
+                    nc.sync.dma_start(
+                        out=g_sc[h][:].bitcast(I32)[r:P:32, :, :],
+                        in_=g_scale_rows[r][:, :, N * h : N * (h + 1)].bitcast(I32),
+                    )
+            elif name[0] == "g":
+                h, g = int(name[1]), int(name[2])
+                nc.sync.dma_start(
+                    out=g_codes[h][:, g, :].bitcast(I32),
+                    in_=g_by_part[:, g, 4 * N * h : 4 * N * (h + 1)].bitcast(I32),
+                )
+            elif name[0] == "G":
+                h = int(name[1])
+                nc.sync.dma_start(
+                    out=g_codes[h][:].bitcast(I32),
+                    in_=g_by_part[:, :, 4 * N * h : 4 * N * (h + 1)].bitcast(I32),
+                )
+            else:
+                t = name[:2]
+                if t not in raw:
+                    raw[t] = keep.tile([P, S], BF16, name="raw" + t, align_bytes=64)
+                cols = slice(0, S) if len(name) == 2 else slice(0, S // 2) if name[2] == "a" else slice(S // 2, S)
+                nc.sync.dma_start(out=raw[t][:, cols], in_=rows[t[0]][int(t[1])][:, cols])
+
+        codes, scales = {}, {}
+        for t in raw:
+            if t[0] != "H":
+                codes[t] = keep.tile([P, PASSES * P], U32, name="c" + t, align_bytes=64)
+                scales[t] = keep.tile([P, PASSES * P], U8, name="s" + t, align_bytes=64)
+
+        halves = [t + b for t in PE_ORDER if len(t) == 2 for b in "01"]
+        re_halves = [x[2:] for x in V_ORDER if x[:2] == "re"]
+        groups = []
+        for x in PE_ORDER:
+            if len(x) == 3 and x[1:] not in groups:
+                groups.append(x[1:])
+        ordered, banks, grouped, acc, drive = {}, {}, {}, {}, {}
+
+        def before(seq, x, depth, prefix):
+            n = seq.index(x)
+            return [prefix + seq[n - depth]] if n >= depth else []
+
+        def needs(op):
+            if op[:2] == "re":
+                return before(re_halves, op[2:], RE_BUFS, "T")
+            if op[0] == "T":
+                first = [] if op[1:3] in DIRECT else ["re" + op[1:]]
+                return first + before(halves, op[1:], T_BANKS, "ev")
+            if op[:2] == "ev":
+                return ["T" + op[2:]] + before(halves, op[2:], GR_BUFS, "q")
+            if op[0] == "q":
+                return ["ev" + op[1:]]
+            if op[0] == "M":
+                t, h = op[1:3], int(op[3])
+                need = ["q" + t + b for b in "01"]
+                if t[0] == "P":
+                    need += ["qH%d%s" % (4 * h + j, b) for j in range(4) for b in "01"]
+                return need + before(groups, op[2:], A_BANKS, "ep")
+            if op[:2] == "ep":
+                return ["MR" + op[2:], "MP" + op[2:], "cal"]
+            if op[:2] == "cl":
+                return ["ep" + op[2:]]
+            return []
+
+        def reorder(x):
+            t, b = x[:2], int(x[2])
+            dst = keep.tile([P, 2 * N], BF16, name="re%d" % (re_halves.index(x) % RE_BUFS), align_bytes=64)
+            src = raw[t][:, 2 * N * b : 2 * N * (b + 1)]
+            if t[0] == "R":
+                nc.vector.tensor_copy(
+                    out=dst[:].bitcast(F32).rearrange("p (u c i) -> p c u i", u=2, i=4),
+                    in_=src.bitcast(F32).rearrange("p (c i u) -> p c u i", u=2, i=4),
+                )
+            else:
+                nc.vector.tensor_copy(
+                    out=dst[:].rearrange("p (u c j) -> p u c j", u=2, j=16),
+                    in_=src.rearrange("p (c u j) -> p u c j", u=2, j=16),
+                )
+            ordered[x] = dst
+
+        def transpose(x):
+            t, b = x[:2], int(x[2])
+            bank = psum.tile([P, 2, 2, P], F32, name="tb%d" % (halves.index(x) % T_BANKS))
+            for g in range(2):
+                for u in range(2):
+                    if t in DIRECT:
+                        first = N * b + 2 * P * g
+                        src = raw[t][:].bitcast(F32)[:, first + u : first + 2 * P : 2]
+                    else:
+                        first = 2 * P * u + P * g
+                        src = ordered[x][:].bitcast(F32)[:, first : first + P]
+                    nc.tensor.transpose(bank[:, g, u, :], src, ident[:])
+            banks[x] = bank
+
+        def evacuate(x, on_vector):
+            dst = keep.tile([P, 2 * N], BF16, name="gr%d" % (halves.index(x) % GR_BUFS), align_bytes=64)
+            dst_words = dst[:].bitcast(F32).rearrange("p (g r u) -> p g r u", g=2, u=2)
+            src = banks[x][:].rearrange("p g u r -> p g r u")
+            if on_vector:
+                nc.vector.tensor_copy(out=dst_words, in_=src)
+            else:
+                nc.scalar.copy(out=dst_words, in_=src)
+            grouped[x] = dst
+
+        def quantise(x):
+            t, b = x[:2], int(x[2])
+            if t[0] == "H":
+                h, j = divmod(int(t[1]), 4)
+                cols = slice(P * j, P * (j + 1))
+                for g in range(2):
+                    nc.vector.quantize_mx(
+                        out=h_codes[h][:, 2 * b + g, cols].bitcast(E4M3X4),
+                        scales=h_sc[h][:, 2 * b + g, cols],
+                        in_=grouped[x][:, N * g : N * (g + 1)],
+                    )
+            else:
+                cols = slice(2 * P * b, 2 * P * (b + 1))
+                nc.vector.quantize_mx(out=codes[t][:, cols].bitcast(E4M3X4), scales=scales[t][:, cols], in_=grouped[x][:])
+
+        def multiply(x):
+            t, h, grp = x[:2], int(x[2]), x[1:]
+            opens = grp not in acc
+            if opens:
+                acc[grp] = psum.tile([P, N], F32, name="ab%d" % (groups.index(grp) % A_BANKS))
+            mov, mov_sc, fmt = (g_codes, g_sc, E5M2X4) if t[0] == "R" else (h_codes, h_sc, E4M3X4)
+            for g in range(PASSES):
+                cols = slice(P * g, P * (g + 1))
+                nc.tensor.matmul_mx(
+                    out=acc[grp][:],
+                    lhsT=codes[t][:, cols].bitcast(E4M3X4),
+                    lhsT_scale=scales[t][:, cols],
+                    rhs=mov[h][:, g, :].bitcast(fmt),
+                    rhs_scale=mov_sc[h][:, g, :],
+                    start=opens and g == 0,
+                    stop=(not opens) and g == PASSES - 1,
+                )
+
+        def calibrate(grp):
+            i = int(grp[0])
+            drive[grp] = keep.tile([P, N], F32, name="dr%d" % (groups.index(grp) % 8))
+            nc.scalar.activation(out=drive[grp][:], in_=acc[grp][:], func=ACT.Copy, scale=cal32[:, i : i + 1])
+
+        def clip(grp):
+            i, h = int(grp[0]), int(grp[1])
+            nc.vector.tensor_scalar(
+                out=drive[grp][:],
+                in0=drive[grp][:],
+                scalar1=vec["lo"][:, i : i + 1],
+                scalar2=vec["hi"][:, i : i + 1],
+                op0=ALU.max,
+                op1=ALU.min,
+            )
+            nc.sync.dma_start(out=out_rows[i][:, N * h : N * (h + 1)], in_=drive[grp][:])
+
+        def emit(op, on_vector):
+            if op == "cal":
+                nc.scalar.activation(out=cal32[:], in_=vec["cal"][:], func=ACT.Copy)
+            elif op[:2] == "re":
+                reorder(op[2:])
+            elif op[0] == "T":
+                transpose(op[1:])
+            elif op[:2] == "ev":
+                evacuate(op[2:], on_vector)
+            elif op[0] == "q":
+                quantise(op[1:])
+            elif op[0] == "M":
+                multiply(op[1:])
+            elif op[:2] == "ep":
+                calibrate(op[2:])
+            else:
+                clip(op[2:])
+
+        pe = []
+        for x in PE_ORDER:
+            pe.extend(["T" + x + "0", "T" + x + "1"] if len(x) == 2 else ["M" + x])
+        queues = [pe, list(S_ORDER), list(V_ORDER)]
+        done = set()
+        for step in range(sum(len(q) for q in queues)):
+            ready = [n for n, q in enumerate(queues) if q and all(d in done for d in needs(q[0]))]
+            op = queues[ready[0]][0]
+            queues[ready[0]].remove(op)
+            emit(op, ready[0] == 2)
+            done.add(op)

@@ -22,14 +22,15 @@ TILES = 8
 N = 512
 T_BANKS = 4
 A_BANKS = 4
-RE_BUFS = 8
+RE_BUFS = 5
 GR_BUFS = 6
+WARM_FIRST = 14
 
-LOADS = "R0a R0b R1 g00 g01 s0 g02 g03 H0 R2 R3 H1 H2 H3 P0 P1 P2 P3 H4 H5 H6 H7 s1 G1 R4 P4 R5 P5 R6 P6 R7 P7".split()
-PE_ORDER = "R0 R1 R00 R10 H0 R2 R3 R20 H1 H2 H3 R30 P0 P1 P2 P00 P3 H4 P10 P20 H5 H6 H7 P30 R01 R11 R21 R4 P4 P01 P11 P21 R31 P31 R5 P5 R40 P40 R41 P41 R6 P6 R50 P50 R51 P51 R7 P7 R60 P60 R61 P61 R70 P70 R71 P71".split()
-DIRECT = set("R0 R1 R2 R3".split())
-V_ORDER = "qR00 qR01 qR10 qR11 reH00 reH01 qH00 qH01 qR20 reH10 qR21 reH11 qR30 reH20 qR31 reH21 reH30 reH31 qH10 reP00 qH11 reP01 qH20 reP10 qH21 qH30 reP11 qH31 reP20 reP21 qP00 reP30 qP01 reP31 qP10 reH40 qP11 reH41 qP20 qP21 reH50 reH51 qP30 reH60 qP31 reH61 qH40 reH70 qH41 reH71 cl00 cl10 cl20 qH50 qH51 qH60 reR40 qH61 reR41 qH70 reP40 qH71 reP41 reR50 reR51 cl30 reP50 reP51 reR60 reR61 qR40 reP60 qR41 reP61 qP40 qP41 cl01 cl11 cl21 reR70 reR71 reP70 qR50 reP71 qR51 cl31 qP50 qP51 cl40 cl41 qR60 qR61 qP60 qP61 cl50 cl51 qR70 qR71 qP70 qP71 cl60 cl61 cl70 cl71".split()
-S_ORDER = "evR00 evR01 cal evR10 evR11 evH00 evH01 evR20 evR21 evR30 evR31 evH10 evH11 evH20 evH21 evH30 evH31 evP00 evP01 evP10 evP11 evP20 evP21 evP30 evP31 evH40 evH41 ep00 ep10 ep20 evH50 evH51 evH60 evH61 evH70 evH71 ep30 evR40 evR41 evP40 evP41 ep01 ep11 ep21 ep31 evR50 evR51 evP50 evP51 ep40 ep41 evR60 evR61 evP60 evP61 ep50 ep51 evR70 evR71 evP70 evP71 ep60 ep61 ep70 ep71".split()
+LOADS = "R0a R0b R1 s0 g00 g01 H0 g02 g03 R2 H1 R3 H2 H3 P0 P1 c P2 P3 s1 H4 H5 G1 H6 H7 R4 P4 R5 P5 R6 P6 R7 P7".split()
+PE_ORDER = "W0 R0 R1 W1 W2 R00a R00b H0 R10a R2 R10b H1 R3 R20a H2 R20b H3 P0 R30a R30b P1 P2 P00a P00b P3 P10a P10b P20a P20b P30a P30b H4 H5 R01a R01b R11a R11b H6 H7 R21a R21b R31a R31b R4 P4 P01a P01b P11a P11b P21a P21b P31a P31b R5 P5 R40a R40b P40a P40b R41a R41b P41a P41b R6 P6 R50a R50b P50a P50b R51a R51b P51a P51b R7 P7 R60a R60b P60a P60b R61a R61b P61a P61b R70a R70b P70a P70b R71a R71b P71a P71b".split()
+DIRECT = set("R0 R1 R3".split())
+V_ORDER = "qR00 qR01 qR10 qR11 reH00 reH01 reR20 reR21 qH00 reH10 qH01 reH11 qR20 qR21 reH20 qH10 reH21 qH11 qR30 reH30 qR31 reH31 reP00 qH20 reP01 qH21 reP10 qH30 reP11 qH31 reP20 qP00 reP21 qP01 reP30 reP31 qP10 qP11 reH40 qP20 reH41 qP21 reH50 reH51 qP30 cl00 qP31 cl10 reH60 cl20 reH61 reH70 reH71 qH40 reR40 qH41 qH50 cl30 qH51 reR41 reP40 reP41 qH60 qH61 reR50 qH70 qH71 reR51 reP50 reP51 qR40 qR41 reR60 qP40 qP41 cl01 cl11 cl21 reR61 reP60 reP61 qR50 reR70 qR51 qP50 cl31 qP51 cl40 reR71 reP70 reP71 qR60 qR61 cl41 qP60 qP61 cl50 cl51 qR70 qR71 qP70 qP71 cl60 cl61 cl70 cl71".split()
+S_ORDER = "cal evR00 evR01 evR10 evR11 evH00 evH01 evR20 evR21 evH10 evH11 evR30 evR31 evH20 evH21 evH30 evH31 evP00 evP01 evP10 evP11 evP20 evP21 ep00 evP30 evP31 ep10 ep20 ep30 evH40 evH41 evH50 evH51 evH60 evH61 evH70 evH71 evR40 evR41 evP40 evP41 ep01 ep11 ep21 ep31 evR50 evR51 evP50 evP51 ep40 ep41 evR60 evR61 evP60 evP61 ep50 ep51 evR70 evR71 evP70 evP71 ep60 ep61 ep70 ep71".split()
 
 
 def tile_adaptive_optics_reconstructor_e4_kernel(tc, rec, g_words, g_scales, pred, hist, cal, lo, hi, out):
@@ -50,10 +51,15 @@ def tile_adaptive_optics_reconstructor_e4_kernel(tc, rec, g_words, g_scales, pre
 
         ident = keep.tile([P, P], F32, name="ident")
         make_identity(nc, ident[:])
-        vec = {}
+        vec, vec_src = {}, {}
         for key, src in (("cal", cal), ("lo", lo), ("hi", hi)):
             vec[key] = keep.tile([P, TILES], BF16, name=key)
-            nc.gpsimd.dma_start(out=vec[key][:], in_=src.rearrange("(p i) -> p i", i=TILES))
+            vec_src[key] = src.rearrange("(p i) -> p i", i=TILES)
+        nc.scalar.dma_start(out=vec["cal"][:], in_=vec_src["cal"])
+        warm_in = keep.tile([P, N], BF16, name="warm_in", align_bytes=64)
+        warm_codes = keep.tile([P, P], U32, name="warm_codes", align_bytes=64)
+        warm_sc = keep.tile([P, P], U8, name="warm_sc", align_bytes=64)
+        nc.vector.memset(warm_in[:].bitcast(U32), 0)
         cal32 = keep.tile([P, TILES], F32, name="cal32")
 
         g_codes, g_sc, h_codes, h_sc = [], [], [], []
@@ -63,10 +69,15 @@ def tile_adaptive_optics_reconstructor_e4_kernel(tc, rec, g_words, g_scales, pre
             h_codes.append(keep.tile([P, PASSES, N], U32, name="hc%d" % h, align_bytes=64))
             h_sc.append(keep.tile([P, PASSES, N], U8, name="hs%d" % h, align_bytes=64))
             nc.vector.memset(g_sc[h][:].bitcast(U32), 0)
+            if h == 0:
+                nc.vector.quantize_mx(out=warm_codes[:].bitcast(E4M3X4), scales=warm_sc[:], in_=warm_in[:])
 
         raw = {}
         for name in LOADS:
-            if name[0] == "s":
+            if name == "c":
+                for key in ("lo", "hi"):
+                    nc.sync.dma_start(out=vec[key][:], in_=vec_src[key])
+            elif name[0] == "s":
                 h = int(name[1])
                 for r in range(4):
                     nc.sync.dma_start(
@@ -98,13 +109,13 @@ def tile_adaptive_optics_reconstructor_e4_kernel(tc, rec, g_words, g_scales, pre
                 codes[t] = keep.tile([P, PASSES * P], U32, name="c" + t, align_bytes=64)
                 scales[t] = keep.tile([P, PASSES * P], U8, name="s" + t, align_bytes=64)
 
-        halves = [t + b for t in PE_ORDER if len(t) == 2 for b in "01"]
+        halves = [t + b for t in PE_ORDER if len(t) == 2 and t[0] != "W" for b in "01"]
         re_halves = [x[2:] for x in V_ORDER if x[:2] == "re"]
         groups = []
         for x in PE_ORDER:
-            if len(x) == 3 and x[1:] not in groups:
-                groups.append(x[1:])
-        ordered, banks, grouped, acc, drive = {}, {}, {}, {}, {}
+            if len(x) == 4 and x[1:3] not in groups:
+                groups.append(x[1:3])
+        ordered, banks, grouped, acc, drive, count = {}, {}, {}, {}, {}, {}
 
         def before(seq, x, depth, prefix):
             n = seq.index(x)
@@ -125,9 +136,9 @@ def tile_adaptive_optics_reconstructor_e4_kernel(tc, rec, g_words, g_scales, pre
                 need = ["q" + t + b for b in "01"]
                 if t[0] == "P":
                     need += ["qH%d%s" % (4 * h + j, b) for j in range(4) for b in "01"]
-                return need + before(groups, op[2:], A_BANKS, "ep")
+                return need + before(groups, op[2:4], A_BANKS, "ep")
             if op[:2] == "ep":
-                return ["MR" + op[2:], "MP" + op[2:], "cal"]
+                return ["MR" + op[2:] + "b", "MP" + op[2:] + "b", "cal"]
             if op[:2] == "cl":
                 return ["ep" + op[2:]]
             return []
@@ -188,45 +199,66 @@ def tile_adaptive_optics_reconstructor_e4_kernel(tc, rec, g_words, g_scales, pre
                 nc.vector.quantize_mx(out=codes[t][:, cols].bitcast(E4M3X4), scales=scales[t][:, cols], in_=grouped[x][:])
 
         def multiply(x):
-            t, h, grp = x[:2], int(x[2]), x[1:]
-            opens = grp not in acc
-            if opens:
+            t, h, grp = x[:2], int(x[2]), x[1:3]
+            if grp not in acc:
+                count[grp] = 0
                 acc[grp] = psum.tile([P, N], F32, name="ab%d" % (groups.index(grp) % A_BANKS))
             mov, mov_sc, fmt = (g_codes, g_sc, E5M2X4) if t[0] == "R" else (h_codes, h_sc, E4M3X4)
-            for g in range(PASSES):
+            for g in (0, 1) if x[3] == "a" else (2, 3):
                 cols = slice(P * g, P * (g + 1))
+                count[grp] = count[grp] + 1
                 nc.tensor.matmul_mx(
                     out=acc[grp][:],
                     lhsT=codes[t][:, cols].bitcast(E4M3X4),
                     lhsT_scale=scales[t][:, cols],
                     rhs=mov[h][:, g, :].bitcast(fmt),
                     rhs_scale=mov_sc[h][:, g, :],
-                    start=opens and g == 0,
-                    stop=(not opens) and g == PASSES - 1,
+                    start=count[grp] == 1,
+                    stop=count[grp] == 2 * PASSES,
                 )
+
+        def warm(x):
+            bank = psum.tile([P, N], F32, name="ab%d" % (A_BANKS - 1))
+            for n in range(WARM_FIRST if x == "W0" else 4):
+                nc.tensor.matmul_mx(
+                    out=bank[:, P * (n % 4) : P * (n % 4 + 1)],
+                    lhsT=warm_codes[:].bitcast(E4M3X4),
+                    lhsT_scale=warm_sc[:],
+                    rhs=warm_codes[:].bitcast(E4M3X4),
+                    rhs_scale=warm_sc[:],
+                    start=True,
+                    stop=True,
+                )
+
+        def pieces(grp):
+            return [slice(0, N // 2), slice(N // 2, N)] if grp == groups[-1] else [slice(0, N)]
 
         def calibrate(grp):
             i = int(grp[0])
             drive[grp] = keep.tile([P, N], F32, name="dr%d" % (groups.index(grp) % 8))
-            nc.scalar.activation(out=drive[grp][:], in_=acc[grp][:], func=ACT.Copy, scale=cal32[:, i : i + 1])
+            for cols in pieces(grp):
+                nc.scalar.activation(out=drive[grp][:, cols], in_=acc[grp][:, cols], func=ACT.Copy, scale=cal32[:, i : i + 1])
 
         def clip(grp):
             i, h = int(grp[0]), int(grp[1])
-            nc.vector.tensor_scalar(
-                out=drive[grp][:],
-                in0=drive[grp][:],
-                scalar1=vec["lo"][:, i : i + 1],
-                scalar2=vec["hi"][:, i : i + 1],
-                op0=ALU.max,
-                op1=ALU.min,
-            )
-            nc.sync.dma_start(out=out_rows[i][:, N * h : N * (h + 1)], in_=drive[grp][:])
+            for cols in pieces(grp):
+                nc.vector.tensor_scalar(
+                    out=drive[grp][:, cols],
+                    in0=drive[grp][:, cols],
+                    scalar1=vec["lo"][:, i : i + 1],
+                    scalar2=vec["hi"][:, i : i + 1],
+                    op0=ALU.max,
+                    op1=ALU.min,
+                )
+                nc.sync.dma_start(out=out_rows[i][:, N * h : N * (h + 1)][:, cols], in_=drive[grp][:, cols])
 
         def emit(op, on_vector):
             if op == "cal":
                 nc.scalar.activation(out=cal32[:], in_=vec["cal"][:], func=ACT.Copy)
             elif op[:2] == "re":
                 reorder(op[2:])
+            elif op[0] == "W":
+                warm(op)
             elif op[0] == "T":
                 transpose(op[1:])
             elif op[:2] == "ev":
@@ -242,7 +274,7 @@ def tile_adaptive_optics_reconstructor_e4_kernel(tc, rec, g_words, g_scales, pre
 
         pe = []
         for x in PE_ORDER:
-            pe.extend(["T" + x + "0", "T" + x + "1"] if len(x) == 2 else ["M" + x])
+            pe.extend([x] if x[0] == "W" else ["T" + x + "0", "T" + x + "1"] if len(x) == 2 else ["M" + x])
         queues = [pe, list(S_ORDER), list(V_ORDER)]
         done = set()
         for step in range(sum(len(q) for q in queues)):

@@ -22,15 +22,16 @@ TILES = 8
 N = 512
 T_BANKS = 4
 A_BANKS = 4
-RE_BUFS = 5
-GR_BUFS = 6
+RE_BUFS = 6
+GR_BUFS = 8
+SHARED = "R4 P4 R5 P5 R6 P6".split()
 WARM_FIRST = 14
 
-LOADS = "R0a R0b R1 s0 g00 g01 H0 g02 g03 R2 H1 R3 H2 H3 P0 P1 c P2 P3 s1 H4 H5 G1 H6 H7 R4 P4 R5 P5 R6 P6 R7 P7".split()
-PE_ORDER = "W0 R0 R1 W1 W2 R00a R00b H0 R10a R2 R10b H1 R3 R20a H2 R20b H3 P0 R30a R30b P1 P2 P00a P00b P3 P10a P10b P20a P20b P30a P30b H4 H5 R01a R01b R11a R11b H6 H7 R21a R21b R31a R31b R4 P4 P01a P01b P11a P11b P21a P21b P31a P31b R5 P5 R40a R40b P40a P40b R41a R41b P41a P41b R6 P6 R50a R50b P50a P50b R51a R51b P51a P51b R7 P7 R60a R60b P60a P60b R61a R61b P61a P61b R70a R70b P70a P70b R71a R71b P71a P71b".split()
-DIRECT = set("R0 R1 R3".split())
-V_ORDER = "qR00 qR01 qR10 qR11 reH00 reH01 reR20 reR21 qH00 reH10 qH01 reH11 qR20 qR21 reH20 qH10 reH21 qH11 qR30 reH30 qR31 reH31 reP00 qH20 reP01 qH21 reP10 qH30 reP11 qH31 reP20 qP00 reP21 qP01 reP30 reP31 qP10 qP11 reH40 qP20 reH41 qP21 reH50 reH51 qP30 cl00 qP31 cl10 reH60 cl20 reH61 reH70 reH71 qH40 reR40 qH41 qH50 cl30 qH51 reR41 reP40 reP41 qH60 qH61 reR50 qH70 qH71 reR51 reP50 reP51 qR40 qR41 reR60 qP40 qP41 cl01 cl11 cl21 reR61 reP60 reP61 qR50 reR70 qR51 qP50 cl31 qP51 cl40 reR71 reP70 reP71 qR60 qR61 cl41 qP60 qP61 cl50 cl51 qR70 qR71 qP70 qP71 cl60 cl61 cl70 cl71".split()
-S_ORDER = "cal evR00 evR01 evR10 evR11 evH00 evH01 evR20 evR21 evH10 evH11 evR30 evR31 evH20 evH21 evH30 evH31 evP00 evP01 evP10 evP11 evP20 evP21 ep00 evP30 evP31 ep10 ep20 ep30 evH40 evH41 evH50 evH51 evH60 evH61 evH70 evH71 evR40 evR41 evP40 evP41 ep01 ep11 ep21 ep31 evR50 evR51 evP50 evP51 ep40 ep41 evR60 evR61 evP60 evP61 ep50 ep51 evR70 evR71 evP70 evP71 ep60 ep61 ep70 ep71".split()
+LOADS = "R0a R0b R1 g00+g01 s0 H0 R2 g02+g03 R3 H1 H2 H3 P0 P1 c P2 P3 H4 s1 H5 H6 G1 H7 R4 P4 R5 P5 R6 P6 R7 P7".split()
+PE_ORDER = "W0 R0 R1 R00a R10a R2 H0 R00b R10b R3 H1 R20a R20b H2 R30a H3 P0 R30b P1 P2 P00a P00b P10a P3 H4 P10b P20a P20b H5 H6 P30a P30b R01a R01b R11a R11b H7 R4 P4 R21a R21b R31a R31b P01a P01b P11a P11b P21a P21b P31a P31b R5 P5 R6 R40a R40b R41a R41b P40a P40b P41a P41b P6 R7 P7 R50a R50b R51a R51b P50a P50b P51a P51b R60a R60b R61a R61b P60a P60b P61a P61b R70a R70b P70a P70b R71a R71b P71a P71b".split()
+DIRECT = set("R2 R3".split())
+V_ORDER = "reR00 reR01 reR10 qR00 reR11 qR01 qR10 qR11 reH00 reH01 qR20 qR21 qH00 qH01 reH10 reH11 reH20 qR30 reH21 qR31 reH30 qH10 qH11 reH31 reP00 reP01 qH20 reP10 qH21 reP11 reP20 qH30 qH31 reP21 qP00 reP30 qP01 qP10 reP31 qP11 reH40 qP20 reH41 qP21 reH50 reH51 reH60 qP30 reH61 qP31 qH40 qH41 reH70 qH50 reH71 qH51 reR40 qH60 qH61 reR41 reP40 reP41 reR50 reR51 reP50 qH70 qH71 reP51 qR40 reR60 qR41 reR61 qP40 qP41 cl00 cl10 cl20 cl30 cl01 reP60 reP61 reR70 qR50 reR71 qR51 reP70 qP50 qP51 reP71 qR60 qR61 cl11 cl21 cl31 qP60 qP61 qR70 qR71 qP70 qP71 cl40 cl41 cl50 cl51 cl60 cl61 cl70 cl71".split()
+S_ORDER = "cal evR00 evR01 evR10 evR11 evR20 evR21 evH00 evH01 evR30 evR31 evH10 evH11 evH20 evH21 evH30 evH31 evP00 evP01 evP10 evP11 evP20 evP21 ep00 evP30 evP31 evH40 evH41 ep10 ep20 evH50 evH51 evH60 evH61 ep30 evH70 evH71 evR40 evR41 evP40 evP41 ep01 ep11 ep21 ep31 evR50 evR51 evP50 evP51 evR60 evR61 ep40 ep41 evP60 evP61 evR70 evR71 evP70 evP71 ep50 ep51 ep60 ep61 ep70 ep71".split()
 
 
 def tile_adaptive_optics_reconstructor_e4_kernel(tc, rec, g_words, g_scales, pred, hist, cal, lo, hi, out):
@@ -85,7 +86,7 @@ def tile_adaptive_optics_reconstructor_e4_kernel(tc, rec, g_words, g_scales, pre
                         in_=g_scale_rows[r][:, :, N * h : N * (h + 1)].bitcast(I32),
                     )
             elif name[0] == "g":
-                h, g = int(name[1]), int(name[2])
+                h, g = int(name[1]), slice(int(name[2]), int(name[-1]) + 1)
                 nc.sync.dma_start(
                     out=g_codes[h][:, g, :].bitcast(I32),
                     in_=g_by_part[:, g, 4 * N * h : 4 * N * (h + 1)].bitcast(I32),
@@ -115,18 +116,37 @@ def tile_adaptive_optics_reconstructor_e4_kernel(tc, rec, g_words, g_scales, pre
         for x in PE_ORDER:
             if len(x) == 4 and x[1:3] not in groups:
                 groups.append(x[1:3])
+        free = [(n, None) for n in range(8)]
+        bank_of, bank_after, seen = {}, {}, {}
+        for x in PE_ORDER:
+            if x[0] == "W":
+                continue
+            for user in [x + "0", x + "1"] if len(x) == 2 else [x[1:3]]:
+                if user not in bank_of:
+                    bank_of[user], bank_after[user] = free[0]
+                    free.remove(free[0])
+                seen[user] = seen.get(user, 0) + 1
+                if len(x) == 2:
+                    free.append((bank_of[user], "ev" + user))
+                elif seen[user] == 4:
+                    free.append((bank_of[user], "ep" + user))
         ordered, banks, grouped, acc, drive, count = {}, {}, {}, {}, {}, {}
 
         def before(seq, x, depth, prefix):
             n = seq.index(x)
             return [prefix + seq[n - depth]] if n >= depth else []
 
+        def freed(user):
+            return [bank_after[user]] if bank_after[user] else []
+
         def needs(op):
+            if op[0] == "B":
+                return needs("M" + op[1:] + "0a") + needs("M" + op[1:] + "1a")
             if op[:2] == "re":
                 return before(re_halves, op[2:], RE_BUFS, "T")
             if op[0] == "T":
                 first = [] if op[1:3] in DIRECT else ["re" + op[1:]]
-                return first + before(halves, op[1:], T_BANKS, "ev")
+                return first + freed(op[1:])
             if op[:2] == "ev":
                 return ["T" + op[2:]] + before(halves, op[2:], GR_BUFS, "q")
             if op[0] == "q":
@@ -136,7 +156,7 @@ def tile_adaptive_optics_reconstructor_e4_kernel(tc, rec, g_words, g_scales, pre
                 need = ["q" + t + b for b in "01"]
                 if t[0] == "P":
                     need += ["qH%d%s" % (4 * h + j, b) for j in range(4) for b in "01"]
-                return need + before(groups, op[2:4], A_BANKS, "ep")
+                return need + freed(op[2:4])
             if op[:2] == "ep":
                 return ["MR" + op[2:] + "b", "MP" + op[2:] + "b", "cal"]
             if op[:2] == "cl":
@@ -161,7 +181,7 @@ def tile_adaptive_optics_reconstructor_e4_kernel(tc, rec, g_words, g_scales, pre
 
         def transpose(x):
             t, b = x[:2], int(x[2])
-            bank = psum.tile([P, 2, 2, P], F32, name="tb%d" % (halves.index(x) % T_BANKS))
+            bank = psum.tile([P, 2, 2, P], F32, name="bank%d" % bank_of[x])
             for g in range(2):
                 for u in range(2):
                     if t in DIRECT:
@@ -198,13 +218,13 @@ def tile_adaptive_optics_reconstructor_e4_kernel(tc, rec, g_words, g_scales, pre
                 cols = slice(2 * P * b, 2 * P * (b + 1))
                 nc.vector.quantize_mx(out=codes[t][:, cols].bitcast(E4M3X4), scales=scales[t][:, cols], in_=grouped[x][:])
 
-        def multiply(x):
+        def multiply(x, passes):
             t, h, grp = x[:2], int(x[2]), x[1:3]
             if grp not in acc:
                 count[grp] = 0
-                acc[grp] = psum.tile([P, N], F32, name="ab%d" % (groups.index(grp) % A_BANKS))
+                acc[grp] = psum.tile([P, N], F32, name="bank%d" % bank_of[grp])
             mov, mov_sc, fmt = (g_codes, g_sc, E5M2X4) if t[0] == "R" else (h_codes, h_sc, E4M3X4)
-            for g in (0, 1) if x[3] == "a" else (2, 3):
+            for g in passes:
                 cols = slice(P * g, P * (g + 1))
                 count[grp] = count[grp] + 1
                 nc.tensor.matmul_mx(
@@ -218,7 +238,7 @@ def tile_adaptive_optics_reconstructor_e4_kernel(tc, rec, g_words, g_scales, pre
                 )
 
         def warm(x):
-            bank = psum.tile([P, N], F32, name="ab%d" % (A_BANKS - 1))
+            bank = psum.tile([P, N], F32, name="bank7")
             for n in range(WARM_FIRST if x == "W0" else 4):
                 nc.tensor.matmul_mx(
                     out=bank[:, P * (n % 4) : P * (n % 4 + 1)],
@@ -266,7 +286,13 @@ def tile_adaptive_optics_reconstructor_e4_kernel(tc, rec, g_words, g_scales, pre
             elif op[0] == "q":
                 quantise(op[1:])
             elif op[0] == "M":
-                multiply(op[1:])
+                multiply(op[1:], (0, 1) if op[4] == "a" else (2, 3))
+            elif op[0] == "B":
+                for g in range(PASSES):
+                    for h in "01":
+                        multiply(op[1:] + h, (g,))
+                for h in "01":
+                    done.add("M" + op[1:] + h + "b")
             elif op[:2] == "ep":
                 calibrate(op[2:])
             else:
@@ -274,6 +300,10 @@ def tile_adaptive_optics_reconstructor_e4_kernel(tc, rec, g_words, g_scales, pre
 
         pe = []
         for x in PE_ORDER:
+            if len(x) == 4 and x[:2] in SHARED:
+                if x[2:] == "0a":
+                    pe.append("B" + x[:2])
+                continue
             pe.extend([x] if x[0] == "W" else ["T" + x + "0", "T" + x + "1"] if len(x) == 2 else ["M" + x])
         queues = [pe, list(S_ORDER), list(V_ORDER)]
         done = set()

@@ -24,14 +24,14 @@ T_BANKS = 4
 A_BANKS = 4
 RE_BUFS = 6
 GR_BUFS = 8
-SHARED = "R4 P4 R5 P5 R6 P6".split()
+SHARED = "R4 P4 R5 P5 R6 P6 R7".split()
 WARM_FIRST = 14
 
-LOADS = "R0a R0b R1 g00+g01 s0 H0 R2 g02+g03 R3 H1 H2 H3 P0 P1 c P2 P3 H4 s1 H5 H6 G1 H7 R4 P4 R5 P5 R6 P6 R7 P7".split()
-PE_ORDER = "W0 R0 R1 R00a R10a R2 H0 R00b R10b R3 H1 R20a R20b H2 R30a H3 P0 R30b P1 P2 P00a P00b P10a P3 H4 P10b P20a P20b H5 H6 P30a P30b R01a R01b R11a R11b H7 R4 P4 R21a R21b R31a R31b P01a P01b P11a P11b P21a P21b P31a P31b R5 P5 R6 R40a R40b R41a R41b P40a P40b P41a P41b P6 R7 P7 R50a R50b R51a R51b P50a P50b P51a P51b R60a R60b R61a R61b P60a P60b P61a P61b R70a R70b P70a P70b R71a R71b P71a P71b".split()
-DIRECT = set("R2 R3".split())
-V_ORDER = "reR00 reR01 reR10 qR00 reR11 qR01 qR10 qR11 reH00 reH01 qR20 qR21 qH00 qH01 reH10 reH11 reH20 qR30 reH21 qR31 reH30 qH10 qH11 reH31 reP00 reP01 qH20 reP10 qH21 reP11 reP20 qH30 qH31 reP21 qP00 reP30 qP01 qP10 reP31 qP11 reH40 qP20 reH41 qP21 reH50 reH51 reH60 qP30 reH61 qP31 qH40 qH41 reH70 qH50 reH71 qH51 reR40 qH60 qH61 reR41 reP40 reP41 reR50 reR51 reP50 qH70 qH71 reP51 qR40 reR60 qR41 reR61 qP40 qP41 cl00 cl10 cl20 cl30 cl01 reP60 reP61 reR70 qR50 reR71 qR51 reP70 qP50 qP51 reP71 qR60 qR61 cl11 cl21 cl31 qP60 qP61 qR70 qR71 qP70 qP71 cl40 cl41 cl50 cl51 cl60 cl61 cl70 cl71".split()
-S_ORDER = "cal evR00 evR01 evR10 evR11 evR20 evR21 evH00 evH01 evR30 evR31 evH10 evH11 evH20 evH21 evH30 evH31 evP00 evP01 evP10 evP11 evP20 evP21 ep00 evP30 evP31 evH40 evH41 ep10 ep20 evH50 evH51 evH60 evH61 ep30 evH70 evH71 evR40 evR41 evP40 evP41 ep01 ep11 ep21 ep31 evR50 evR51 evP50 evP51 evR60 evR61 ep40 ep41 evP60 evP61 evR70 evR71 evP70 evP71 ep50 ep51 ep60 ep61 ep70 ep71".split()
+LOADS = "R0a R0b R1 R2 R3 g00+g01 s0 H0 H1 H2 g02+g03 H3 P0 P1 c P2 P3 H4 s1 H5 H6 G1 H7 R4 P4 R5 P5 R6 P6 R7 P7".split()
+PE_ORDER = "W0 R0 W1 W2 R1 W3 R2 R3 R00a R10a W4 W5 W6 R20a H0 H1 R30a H2 R00b R10b R20b H3 P0 R30b P1 P2 P00a P00b P10a P10b P3 H4 H5 H6 P20a P20b P30a P30b R01a R01b R11a R11b H7 R4 P4 R21a R21b R31a R31b P01a P01b P11a P11b P21a P21b P31a P31b R5 P5 R6 R40a R40b R41a R41b P40a P40b P41a P41b P6 R7 P7 R50a R50b R51a R51b P50a P50b P51a P51b R60a R60b R61a R61b P60a P60b P61a P61b R70a R70b R71a R71b P70a P70b P71a P71b".split()
+DIRECT = set("".split())
+V_ORDER = "reR00 reR01 reR10 qR00 reR11 qR01 reR20 reR21 qR10 reR30 qR11 reR31 qR20 qR21 qR30 qR31 reH00 reH01 reH10 reH11 reH20 reH21 qH00 qH01 qH10 reH30 qH11 qH20 reH31 qH21 reP00 reP01 reP10 reP11 qH30 reP20 qH31 reP21 qP00 qP01 reP30 qP10 reP31 qP11 reH40 qP20 reH41 qP21 reH50 reH51 reH60 reH61 qP30 qP31 qH40 qH41 qH50 qH51 reH70 qH60 reH71 qH61 reR40 reR41 reP40 reP41 reR50 reR51 qH70 reP50 qH71 reP51 qR40 qR41 reR60 qP40 reR61 qP41 cl00 cl10 cl20 cl30 cl01 reP60 reP61 reR70 qR50 reR71 qR51 reP70 qP50 qP51 reP71 qR60 qR61 cl11 cl21 cl31 qP60 qP61 qR70 qR71 qP70 qP71 cl40 cl41 cl50 cl51 cl60 cl61 cl70 cl71".split()
+S_ORDER = "cal evR00 evR01 evR10 evR11 evR20 evR21 evR30 evR31 evH00 evH01 evH10 evH11 evH20 evH21 evH30 evH31 evP00 evP01 evP10 evP11 evP20 evP21 ep00 ep10 evP30 evP31 evH40 evH41 evH50 evH51 evH60 evH61 ep20 ep30 evH70 evH71 evR40 evR41 evP40 evP41 ep01 ep11 ep21 ep31 evR50 evR51 evP50 evP51 evR60 evR61 ep40 ep41 evP60 evP61 evR70 evR71 evP70 evP71 ep50 ep51 ep60 ep61 ep70 ep71".split()
 
 
 def tile_adaptive_optics_reconstructor_e4_kernel(tc, rec, g_words, g_scales, pred, hist, cal, lo, hi, out):
@@ -120,6 +120,7 @@ def tile_adaptive_optics_reconstructor_e4_kernel(tc, rec, g_words, g_scales, pre
         bank_of, bank_after, seen = {}, {}, {}
         for x in PE_ORDER:
             if x[0] == "W":
+                bank_of[x], bank_after[x] = free[1]
                 continue
             for user in [x + "0", x + "1"] if len(x) == 2 else [x[1:3]]:
                 if user not in bank_of:
@@ -140,6 +141,8 @@ def tile_adaptive_optics_reconstructor_e4_kernel(tc, rec, g_words, g_scales, pre
             return [bank_after[user]] if bank_after[user] else []
 
         def needs(op):
+            if op[0] == "W":
+                return freed(op)
             if op[0] == "B":
                 return needs("M" + op[1:] + "0a") + needs("M" + op[1:] + "1a")
             if op[:2] == "re":
@@ -238,7 +241,7 @@ def tile_adaptive_optics_reconstructor_e4_kernel(tc, rec, g_words, g_scales, pre
                 )
 
         def warm(x):
-            bank = psum.tile([P, N], F32, name="bank7")
+            bank = psum.tile([P, N], F32, name="bank%d" % bank_of[x])
             for n in range(WARM_FIRST if x == "W0" else 4):
                 nc.tensor.matmul_mx(
                     out=bank[:, P * (n % 4) : P * (n % 4 + 1)],

@@ -50,6 +50,10 @@ def tile_adaptive_optics_reconstructor_e4_kernel(tc, rec, g_words, g_scales, pre
         psum = ctx.enter_context(tc.psum_pool(name="psum", bufs=1))
         ctx.enter_context(tc.manual_schedule())
 
+        def shifted(width, dtype, shift, name):
+            whole = keep.tile([P, shift + width], dtype, name=name, align_bytes=256)
+            return whole[:, shift:]
+
         ident = keep.tile([P, P], F32, name="ident")
         make_identity(nc, ident[:])
         vec, vec_src = {}, {}
@@ -65,10 +69,10 @@ def tile_adaptive_optics_reconstructor_e4_kernel(tc, rec, g_words, g_scales, pre
 
         g_codes, g_sc, h_codes, h_sc = [], [], [], []
         for h in range(2):
-            g_codes.append(keep.tile([P, PASSES, N], U32, name="gc%d" % h, align_bytes=64))
-            g_sc.append(keep.tile([P, PASSES, N], U8, name="gs%d" % h, align_bytes=64))
-            h_codes.append(keep.tile([P, PASSES, N], U32, name="hc%d" % h, align_bytes=64))
-            h_sc.append(keep.tile([P, PASSES, N], U8, name="hs%d" % h, align_bytes=64))
+            g_codes.append(keep.tile([P, PASSES, N], U32, name="gc%d" % h, align_bytes=256))
+            g_sc.append(shifted(PASSES * N, U8, 64, "gs%d" % h).rearrange("p (g n) -> p g n", n=N))
+            h_codes.append(keep.tile([P, PASSES, N], U32, name="hc%d" % h, align_bytes=256))
+            h_sc.append(shifted(PASSES * N, U8, 64, "hs%d" % h).rearrange("p (g n) -> p g n", n=N))
             nc.vector.memset(g_sc[h][:].bitcast(U32), 0)
             if h == 0:
                 nc.vector.quantize_mx(out=warm_codes[:].bitcast(E4M3X4), scales=warm_sc[:], in_=warm_in[:])
@@ -100,15 +104,15 @@ def tile_adaptive_optics_reconstructor_e4_kernel(tc, rec, g_words, g_scales, pre
             else:
                 t = name[:2]
                 if t not in raw:
-                    raw[t] = keep.tile([P, S], BF16, name="raw" + t, align_bytes=64)
+                    raw[t] = keep.tile([P, S], BF16, name="raw%d" % (len(raw) % 20), align_bytes=64)
                 cols = slice(0, S) if len(name) == 2 else slice(0, S // 2) if name[2] == "a" else slice(S // 2, S)
                 nc.sync.dma_start(out=raw[t][:, cols], in_=rows[t[0]][int(t[1])][:, cols])
 
         codes, scales = {}, {}
         for t in raw:
             if t[0] != "H":
-                codes[t] = keep.tile([P, PASSES * P], U32, name="c" + t, align_bytes=64)
-                scales[t] = keep.tile([P, PASSES * P], U8, name="s" + t, align_bytes=64)
+                codes[t] = shifted(PASSES * P, U32, 32, "c" + t)
+                scales[t] = shifted(PASSES * P, U8, 192, "s" + t)
 
         halves = [t + b for t in PE_ORDER if len(t) == 2 and t[0] != "W" for b in "01"]
         re_halves = [x[2:] for x in V_ORDER if x[:2] == "re"]

from contextlib import ExitStack

import concourse.mybir as mybir
from concourse.masks import make_identity

S, A, F, L = 2048, 1024, 1024, 2048
FLOPS = 2 * A * F * (S + L)

F32 = mybir.dt.float32
BF16 = mybir.dt.bfloat16
I32 = mybir.dt.int32
U32 = mybir.dt.uint32
U8 = mybir.dt.uint8
E4M3X4 = mybir.dt.float8_e4m3fn_x4
E5M2X4 = mybir.dt.float8_e5m2_x4
ALU = mybir.AluOpType
ACT = mybir.ActivationFunctionType

P = 128
PASSES = 4
TILES = 8
N = 512
T_BANKS = 4
A_BANKS = 4
RE_BUFS = 6
GR_BUFS = 8
SHARED = "R4 P4 R5 P5 R6 P6 R7".split()
WARM_FIRST = 14

LOADS = "R0a R0b R1 R2 R3 g00+g01 s0 H0 H1 H2 g02+g03 H3 P0 P1 c P2 P3 H4 s1 H5 H6 G1 H7 R4 P4 R5 P5 R6 P6 R7 P7".split()
PE_ORDER = "W0 R0 W1 W2 R1 W3 R2 R3 R00a R10a W4 W5 W6 R20a H0 H1 R30a H2 R00b R10b R20b H3 P0 R30b P1 P2 P00a P00b P10a P10b P3 H4 H5 H6 P20a P20b P30a P30b R01a R01b R11a R11b H7 R4 P4 R21a R21b R31a R31b P01a P01b P11a P11b P21a P21b P31a P31b R5 P5 R6 R40a R40b R41a R41b P40a P40b P41a P41b P6 R7 P7 R50a R50b R51a R51b P50a P50b P51a P51b R60a R60b R61a R61b P60a P60b P61a P61b R70a R70b R71a R71b P70a P70b P71a P71b".split()
DIRECT = set("".split())
V_ORDER = "reR00 reR01 reR10 qR00 reR11 qR01 reR20 reR21 qR10 reR30 qR11 reR31 qR20 qR21 qR30 qR31 reH00 reH01 reH10 reH11 reH20 reH21 qH00 qH01 qH10 reH30 qH11 qH20 reH31 qH21 reP00 reP01 reP10 reP11 qH30 reP20 qH31 reP21 qP00 qP01 reP30 qP10 reP31 qP11 reH40 qP20 reH41 qP21 reH50 reH51 reH60 reH61 qP30 qP31 qH40 qH41 qH50 qH51 reH70 qH60 reH71 qH61 reR40 reR41 reP40 reP41 reR50 reR51 qH70 reP50 qH71 reP51 qR40 qR41 reR60 qP40 reR61 qP41 cl00 cl10 cl20 cl30 cl01 reP60 reP61 reR70 qR50 reR71 qR51 reP70 qP50 qP51 reP71 qR60 qR61 cl11 cl21 cl31 qP60 qP61 qR70 qR71 qP70 qP71 cl40 cl41 cl50 cl51 cl60 cl61 cl70 cl71".split()
S_ORDER = "cal evR00 evR01 evR10 evR11 evR20 evR21 evR30 evR31 evH00 evH01 evH10 evH11 evH20 evH21 evH30 evH31 evP00 evP01 evP10 evP11 evP20 evP21 ep00 ep10 evP30 evP31 evH40 evH41 evH50 evH51 evH60 evH61 ep20 ep30 evH70 evH71 evR40 evR41 evP40 evP41 ep01 ep11 ep21 ep31 evR50 evR51 evP50 evP51 evR60 evR61 ep40 ep41 evP60 evP61 evR70 evR71 evP70 evP71 ep50 ep51 ep60 ep61 ep70 ep71".split()


def tile_adaptive_optics_reconstructor_e4_kernel(tc, rec, g_words, g_scales, pred, hist, cal, lo, hi, out):
    nc = tc.nc
    rows = {
        "R": rec.rearrange("(p i) k -> i p k", i=TILES),
        "P": pred.rearrange("(p i) k -> i p k", i=TILES),
        "H": hist.rearrange("(i p) k -> i p k", p=P),
    }
    out_rows = out.rearrange("(p i) f -> i p f", i=TILES)
    g_by_part = g_words.rearrange("g p n t -> p g (n t)")
    g_scale_rows = g_scales.rearrange("g (q r) n -> r q g n", r=4)

    with ExitStack() as ctx:
        keep = ctx.enter_context(tc.tile_pool(name="keep", bufs=1))
        psum = ctx.enter_context(tc.psum_pool(name="psum", bufs=1))
        ctx.enter_context(tc.manual_schedule())

        def shifted(width, dtype, shift, name):
            whole = keep.tile([P, shift + width], dtype, name=name, align_bytes=256)
            return whole[:, shift:]

        ident = keep.tile([P, P], F32, name="ident")
        make_identity(nc, ident[:])
        vec, vec_src = {}, {}
        for key, src in (("cal", cal), ("lo", lo), ("hi", hi)):
            vec[key] = keep.tile([P, TILES], BF16, name=key)
            vec_src[key] = src.rearrange("(p i) -> p i", i=TILES)
        nc.scalar.dma_start(out=vec["cal"][:], in_=vec_src["cal"])
        warm_in = keep.tile([P, N], BF16, name="warm_in", align_bytes=64)
        warm_codes = keep.tile([P, P], U32, name="warm_codes", align_bytes=64)
        warm_sc = keep.tile([P, P], U8, name="warm_sc", align_bytes=64)
        nc.vector.memset(warm_in[:].bitcast(U32), 0)
        cal32 = keep.tile([P, TILES], F32, name="cal32")

        g_codes, g_sc, h_codes, h_sc = [], [], [], []
        for h in range(2):
            g_codes.append(keep.tile([P, PASSES, N], U32, name="gc%d" % h, align_bytes=256))
            g_sc.append(shifted(PASSES * N, U8, 64, "gs%d" % h).rearrange("p (g n) -> p g n", n=N))
            h_codes.append(keep.tile([P, PASSES, N], U32, name="hc%d" % h, align_bytes=256))
            h_sc.append(shifted(PASSES * N, U8, 64, "hs%d" % h).rearrange("p (g n) -> p g n", n=N))
            nc.vector.memset(g_sc[h][:].bitcast(U32), 0)
            if h == 0:
                nc.vector.quantize_mx(out=warm_codes[:].bitcast(E4M3X4), scales=warm_sc[:], in_=warm_in[:])

        raw = {}
        for name in LOADS:
            if name == "c":
                for key in ("lo", "hi"):
                    nc.sync.dma_start(out=vec[key][:], in_=vec_src[key])
            elif name[0] == "s":
                h = int(name[1])
                for r in range(4):
                    nc.sync.dma_start(
                        out=g_sc[h][:].bitcast(I32)[r:P:32, :, :],
                        in_=g_scale_rows[r][:, :, N * h : N * (h + 1)].bitcast(I32),
                    )
            elif name[0] == "g":
                h, g = int(name[1]), slice(int(name[2]), int(name[-1]) + 1)
                nc.sync.dma_start(
                    out=g_codes[h][:, g, :].bitcast(I32),
                    in_=g_by_part[:, g, 4 * N * h : 4 * N * (h + 1)].bitcast(I32),
                )
            elif name[0] == "G":
                h = int(name[1])
                nc.sync.dma_start(
                    out=g_codes[h][:].bitcast(I32),
                    in_=g_by_part[:, :, 4 * N * h : 4 * N * (h + 1)].bitcast(I32),
                )
            else:
                t = name[:2]
                if t not in raw:
                    raw[t] = keep.tile([P, S], BF16, name="raw%d" % (len(raw) % 20), align_bytes=64)
                cols = slice(0, S) if len(name) == 2 else slice(0, S // 2) if name[2] == "a" else slice(S // 2, S)
                nc.sync.dma_start(out=raw[t][:, cols], in_=rows[t[0]][int(t[1])][:, cols])

        codes, scales = {}, {}
        for t in raw:
            if t[0] != "H":
                codes[t] = shifted(PASSES * P, U32, 32, "c" + t)
                scales[t] = shifted(PASSES * P, U8, 192, "s" + t)

        halves = [t + b for t in PE_ORDER if len(t) == 2 and t[0] != "W" for b in "01"]
        re_halves = [x[2:] for x in V_ORDER if x[:2] == "re"]
        groups = []
        for x in PE_ORDER:
            if len(x) == 4 and x[1:3] not in groups:
                groups.append(x[1:3])
        free = [(n, None) for n in range(8)]
        bank_of, bank_after, seen = {}, {}, {}
        for x in PE_ORDER:
            if x[0] == "W":
                bank_of[x], bank_after[x] = free[1]
                continue
            for user in [x + "0", x + "1"] if len(x) == 2 else [x[1:3]]:
                if user not in bank_of:
                    bank_of[user], bank_after[user] = free[0]
                    free.remove(free[0])
                seen[user] = seen.get(user, 0) + 1
                if len(x) == 2:
                    free.append((bank_of[user], "ev" + user))
                elif seen[user] == 4:
                    free.append((bank_of[user], "ep" + user))
        ordered, banks, grouped, acc, drive, count = {}, {}, {}, {}, {}, {}

        def before(seq, x, depth, prefix):
            n = seq.index(x)
            return [prefix + seq[n - depth]] if n >= depth else []

        def freed(user):
            return [bank_after[user]] if bank_after[user] else []

        def needs(op):
            if op[0] == "W":
                return freed(op)
            if op[0] == "B":
                return needs("M" + op[1:] + "0a") + needs("M" + op[1:] + "1a")
            if op[:2] == "re":
                return before(re_halves, op[2:], RE_BUFS, "T")
            if op[0] == "T":
                first = [] if op[1:3] in DIRECT else ["re" + op[1:]]
                return first + freed(op[1:])
            if op[:2] == "ev":
                return ["T" + op[2:]] + before(halves, op[2:], GR_BUFS, "q")
            if op[0] == "q":
                return ["ev" + op[1:]]
            if op[0] == "M":
                t, h = op[1:3], int(op[3])
                need = ["q" + t + b for b in "01"]
                if t[0] == "P":
                    need += ["qH%d%s" % (4 * h + j, b) for j in range(4) for b in "01"]
                return need + freed(op[2:4])
            if op[:2] == "ep":
                return ["MR" + op[2:] + "b", "MP" + op[2:] + "b", "cal"]
            if op[:2] == "cl":
                return ["ep" + op[2:]]
            return []

        def reorder(x):
            t, b = x[:2], int(x[2])
            dst = keep.tile([P, 2 * N], BF16, name="re%d" % (re_halves.index(x) % RE_BUFS), align_bytes=64)
            src = raw[t][:, 2 * N * b : 2 * N * (b + 1)]
            if t[0] == "R":
                nc.vector.tensor_copy(
                    out=dst[:].bitcast(F32).rearrange("p (u c i) -> p c u i", u=2, i=4),
                    in_=src.bitcast(F32).rearrange("p (c i u) -> p c u i", u=2, i=4),
                )
            else:
                nc.vector.tensor_copy(
                    out=dst[:].rearrange("p (u c j) -> p u c j", u=2, j=16),
                    in_=src.rearrange("p (c u j) -> p u c j", u=2, j=16),
                )
            ordered[x] = dst

        def transpose(x):
            t, b = x[:2], int(x[2])
            bank = psum.tile([P, 2, 2, P], F32, name="bank%d" % bank_of[x])
            for g in range(2):
                for u in range(2):
                    if t in DIRECT:
                        first = N * b + 2 * P * g
                        src = raw[t][:].bitcast(F32)[:, first + u : first + 2 * P : 2]
                    else:
                        first = 2 * P * u + P * g
                        src = ordered[x][:].bitcast(F32)[:, first : first + P]
                    nc.tensor.transpose(bank[:, g, u, :], src, ident[:])
            banks[x] = bank

        def evacuate(x, on_vector):
            dst = keep.tile([P, 2 * N], BF16, name="gr%d" % (halves.index(x) % GR_BUFS), align_bytes=64)
            dst_words = dst[:].bitcast(F32).rearrange("p (g r u) -> p g r u", g=2, u=2)
            src = banks[x][:].rearrange("p g u r -> p g r u")
            if on_vector:
                nc.vector.tensor_copy(out=dst_words, in_=src)
            else:
                nc.scalar.copy(out=dst_words, in_=src)
            grouped[x] = dst

        def quantise(x):
            t, b = x[:2], int(x[2])
            if t[0] == "H":
                h, j = divmod(int(t[1]), 4)
                cols = slice(P * j, P * (j + 1))
                for g in range(2):
                    nc.vector.quantize_mx(
                        out=h_codes[h][:, 2 * b + g, cols].bitcast(E4M3X4),
                        scales=h_sc[h][:, 2 * b + g, cols],
                        in_=grouped[x][:, N * g : N * (g + 1)],
                    )
            else:
                cols = slice(2 * P * b, 2 * P * (b + 1))
                nc.vector.quantize_mx(out=codes[t][:, cols].bitcast(E4M3X4), scales=scales[t][:, cols], in_=grouped[x][:])

        def multiply(x, passes):
            t, h, grp = x[:2], int(x[2]), x[1:3]
            if grp not in acc:
                count[grp] = 0
                acc[grp] = psum.tile([P, N], F32, name="bank%d" % bank_of[grp])
            mov, mov_sc, fmt = (g_codes, g_sc, E5M2X4) if t[0] == "R" else (h_codes, h_sc, E4M3X4)
            for g in passes:
                cols = slice(P * g, P * (g + 1))
                count[grp] = count[grp] + 1
                nc.tensor.matmul_mx(
                    out=acc[grp][:],
                    lhsT=codes[t][:, cols].bitcast(E4M3X4),
                    lhsT_scale=scales[t][:, cols],
                    rhs=mov[h][:, g, :].bitcast(fmt),
                    rhs_scale=mov_sc[h][:, g, :],
                    start=count[grp] == 1,
                    stop=count[grp] == 2 * PASSES,
                )

        def warm(x):
            bank = psum.tile([P, N], F32, name="bank%d" % bank_of[x])
            for n in range(WARM_FIRST if x == "W0" else 4):
                nc.tensor.matmul_mx(
                    out=bank[:, P * (n % 4) : P * (n % 4 + 1)],
                    lhsT=warm_codes[:].bitcast(E4M3X4),
                    lhsT_scale=warm_sc[:],
                    rhs=warm_codes[:].bitcast(E4M3X4),
                    rhs_scale=warm_sc[:],
                    start=True,
                    stop=True,
                )

        def pieces(grp):
            return [slice(0, N // 2), slice(N // 2, N)] if grp == groups[-1] else [slice(0, N)]

        def calibrate(grp):
            i = int(grp[0])
            drive[grp] = keep.tile([P, N], F32, name="dr%d" % (groups.index(grp) % 8))
            for cols in pieces(grp):
                nc.scalar.activation(out=drive[grp][:, cols], in_=acc[grp][:, cols], func=ACT.Copy, scale=cal32[:, i : i + 1])

        def clip(grp):
            i, h = int(grp[0]), int(grp[1])
            for cols in pieces(grp):
                nc.vector.tensor_scalar(
                    out=drive[grp][:, cols],
                    in0=drive[grp][:, cols],
                    scalar1=vec["lo"][:, i : i + 1],
                    scalar2=vec["hi"][:, i : i + 1],
                    op0=ALU.max,
                    op1=ALU.min,
                )
                nc.sync.dma_start(out=out_rows[i][:, N * h : N * (h + 1)][:, cols], in_=drive[grp][:, cols])

        def emit(op, on_vector):
            if op == "cal":
                nc.scalar.activation(out=cal32[:], in_=vec["cal"][:], func=ACT.Copy)
            elif op[:2] == "re":
                reorder(op[2:])
            elif op[0] == "W":
                warm(op)
            elif op[0] == "T":
                transpose(op[1:])
            elif op[:2] == "ev":
                evacuate(op[2:], on_vector)
            elif op[0] == "q":
                quantise(op[1:])
            elif op[0] == "M":
                multiply(op[1:], (0, 1) if op[4] == "a" else (2, 3))
            elif op[0] == "B":
                for g in range(PASSES):
                    for h in "01":
                        multiply(op[1:] + h, (g,))
                for h in "01":
                    done.add("M" + op[1:] + h + "b")
            elif op[:2] == "ep":
                calibrate(op[2:])
            else:
                clip(op[2:])

        pe = []
        for x in PE_ORDER:
            if len(x) == 4 and x[:2] in SHARED:
                if x[2:] == "0a":
                    pe.append("B" + x[:2])
                continue
            pe.extend([x] if x[0] == "W" else ["T" + x + "0", "T" + x + "1"] if len(x) == 2 else ["M" + x])
        queues = [pe, list(S_ORDER), list(V_ORDER)]
        done = set()
        for step in range(sum(len(q) for q in queues)):
            ready = [n for n, q in enumerate(queues) if q and all(d in done for d in needs(q[0]))]
            op = queues[ready[0]][0]
            queues[ready[0]].remove(op)
            emit(op, ready[0] == 2)
            done.add(op)
